import numpy as np
import ml_dtypes


def mxq(x, axis, fmt="e4m3"):
    dtype, down = {"e4m3": (ml_dtypes.float8_e4m3fn, 7), "e5m2": (ml_dtypes.float8_e5m2, 14)}[fmt]
    v = np.moveaxis(np.asarray(x, np.float32).astype(ml_dtypes.bfloat16).astype(np.float64), axis, -1)
    blocks = v.reshape(v.shape[:-1] + (-1, 32))
    amax = np.abs(blocks).max(-1, keepdims=True)
    byte = np.maximum(np.where(amax > 0, np.frexp(amax)[1] - 1 + 127, 0) - down, 1)
    scale = np.exp2(byte - 127.0)
    codes = (blocks / scale).astype(np.float32).astype(dtype).astype(np.float64)
    return np.moveaxis((codes * scale).reshape(v.shape), -1, axis)


WIDE = False


def mx_kscale(k):
    if not WIDE:
        return np.ones(k)
    levels = np.array([10, -10, 5, -5, 0])
    if k % 512:
        return np.exp2(np.random.permutation(np.resize(levels, k // 32))).repeat(32)
    a = np.empty((k // 512, 16))
    for p in range(k // 512):
        a[p, :8] = np.random.permutation(np.resize(levels, 8))
        for g in range(8):
            far = levels[np.abs(levels - a[p, g]) >= 10]
            a[p, g + 8] = far[np.random.randint(len(far))]
    return np.exp2(a.ravel()).repeat(32)


def f64(x):
    return np.asarray(x).astype(np.float64)


def striped8(idx):
    return np.asarray(idx).reshape(8, -1, 16).transpose(0, 2, 1).reshape(128, -1).astype(np.uint16)


def unstriped8(offs):
    return offs.reshape(8, 16, -1).transpose(0, 2, 1).reshape(8, -1).astype(np.int64)


def pick8(x, idx, run):
    r = np.arange(len(x))
    return x[r[:, None], idx[r % (8 * run) // run]]


E2M1 = np.array([0.0, 0.5, 1.0, 1.5, 2.0, 3.0, 4.0, 6.0, -0.0, -0.5, -1.0, -1.5, -2.0, -3.0, -4.0, -6.0])


def pack_weight(w, fmt):
    k, n = w.shape
    w = f64(np.asarray(w, np.float32).astype(ml_dtypes.bfloat16)).reshape(k // 32, 32, n)
    amax = np.abs(w).max(1)
    if fmt == "e4m3":
        byte = np.frexp(amax)[1] - 1 + 127 - 7
    else:
        mant, ex = np.frexp(amax / 6.0)
        byte = np.where(mant > 0.5, ex, ex - 1) + 127
    byte = np.clip(np.where(amax > 0, byte, 1), 1, 254)
    scaled = (w * np.exp2(127.0 - byte)[:, None, :]).reshape(k, n).astype(np.float32)
    by_word = np.ascontiguousarray(scaled.reshape(k // 512, 128, 4, n).transpose(0, 1, 3, 2))
    if fmt == "e4m3":
        words = by_word.astype(ml_dtypes.float8_e4m3fn).view(np.uint8)
    else:
        c = by_word.astype(ml_dtypes.float4_e2m1fn).view(np.uint8) & 0xF
        words = (c[..., 0::2] | (c[..., 1::2] << 4)).reshape(k // 512, 128, 2 * n)
    return np.ascontiguousarray(words), np.ascontiguousarray(byte.astype(np.uint8).reshape(k // 512, 16, n))


def unpack_weight(words, scales, fmt):
    g, _, n = scales.shape
    words = np.ascontiguousarray(words).reshape(g, 128, n, -1)
    if fmt == "e4m3":
        vals = words.view(ml_dtypes.float8_e4m3fn).astype(np.float64)
    else:
        nib = np.empty((g, 128, n, 4), np.uint8)
        nib[..., 0::2] = words & 0xF
        nib[..., 1::2] = words >> 4
        vals = E2M1[nib]
    vals = vals * np.repeat(np.exp2(scales.astype(np.float64) - 127.0), 8, axis=1)[..., None]
    return vals.transpose(0, 1, 3, 2).reshape(g * 512, n)


D, K, T, U, I, Q = 512, 512, 1024, 1024, 512, 128


def setup_inputs():
    n = np.random.standard_normal
    idx = np.stack([np.random.permutation(T)[:I] for _ in range(8)])
    idx2 = np.stack([np.random.permutation(U)[:I] for _ in range(8)])
    idx3 = np.stack([np.random.permutation(U)[:I] for _ in range(8)])
    idx4 = np.stack([np.random.permutation(T)[:I] for _ in range(8)])
    idx5 = np.stack([np.random.permutation(T)[:I] for _ in range(8)])
    fd = mx_kscale(D)
    fk = mx_kscale(K)
    wqp = pack_weight(n((D, K)) * 1.0 / np.sqrt(D) * fd[:, None] * fk, "e4m3")
    keysp = pack_weight(n((K, T)) * 1.0 / np.sqrt(K) / fk[:, None], "e4m3")
    notesp = pack_weight(n((K, U)) * 1.0 / np.sqrt(K) / fk[:, None], "e2m1")
    return {
        "states": (n((D, Q)) * 0.95 / fd[:, None]).astype(np.float32),
        "wq_words": wqp[0],
        "wq_scales": wqp[1],
        "keys_words": keysp[0],
        "keys_scales": keysp[1],
        "notes_words": notesp[0],
        "notes_scales": notesp[1],
        "lam": (np.random.uniform(0.5, 1.5, (Q, 1))).astype(np.float32),
        "offs": striped8(idx),
        "offs2": striped8(idx2),
        "offs3": striped8(idx3),
        "offs4": striped8(idx4),
        "offs5": striped8(idx5),
    }


def reference(states, wq_words, wq_scales, keys_words, keys_scales, notes_words, notes_scales, lam, offs, offs2, offs3, offs4, offs5):
    idx = unstriped8(offs)
    idx2 = unstriped8(offs2)
    idx3 = unstriped8(offs3)
    idx4 = unstriped8(offs4)
    idx5 = unstriped8(offs5)
    wqu = unpack_weight(wq_words, wq_scales, "e4m3")
    keysu = unpack_weight(keys_words, keys_scales, "e4m3")
    notesu = unpack_weight(notes_words, notes_scales, "e2m1")
    statesq = mxq(f64(states), 0, "e4m3")
    qv = wqu.T @ statesq
    qvq = mxq(qv, 0, "e4m3")
    a = qvq.T @ keysu
    b = qvq.T @ notesu
    f1 = np.zeros((Q, U))
    f1[np.arange(Q)[:, None], idx2[np.arange(Q) % 128 // 16]] = pick8(a, idx, 16)
    cc = b + f1
    f2 = np.zeros((Q, T))
    f2[np.arange(Q)[:, None], idx4[np.arange(Q) % 128 // 16]] = pick8(cc, idx3, 16)
    dd = a + f2 * f64(lam)
    y = pick8(dd, idx5, 16)
    return y

@@ -1,0 +1,167 @@
+from contextlib import ExitStack
+
+import concourse.mybir as mybir
+
+D, K, T, U, SLOTS, Q = 512, 512, 1024, 1024, 512, 128
+FLOPS = 2 * Q * (D * K + K * T + K * U)
+
+F32 = mybir.dt.float32
+BF16 = mybir.dt.bfloat16
+I32 = mybir.dt.int32
+U32 = mybir.dt.uint32
+U16 = mybir.dt.uint16
+U8 = mybir.dt.uint8
+FP8X4 = mybir.dt.float8_e4m3fn_x4
+FP4X4 = mybir.dt.float4_e2m1fn_x4
+COPY = mybir.ActivationFunctionType.Copy
+MULT = mybir.AluOpType.mult
+ADD = mybir.AluOpType.add
+
+P = 128
+PACK = 4
+HALF = SLOTS // 2
+HALF_COLS = HALF // 16
+A_COLS = 256
+B_COLS = 512
+STATES_ON_VECTOR = 96
+
+
+def load_scale_rows(queue, plane, scales):
+    for quad in range(4):
+        queue.dma_start(
+            out=plane[32 * quad : 32 * quad + 4, :].bitcast(I32),
+            in_=scales[0, 4 * quad : 4 * quad + 4, :].bitcast(I32),
+        )
+
+
+def tile_attend_thereandback_madetwo_kernel(
+    tc, states, wq_words, wq_scales, keys_words, keys_scales, notes_words, notes_scales, lam, offs, offs2, offs3, offs4, offs5, out
+):
+    nc = tc.nc
+    with ExitStack() as ctx:
+        sb = ctx.enter_context(tc.tile_pool(name="sb", bufs=1))
+        ps = ctx.enter_context(tc.psum_pool(name="ps", bufs=1))
+
+        wq_plane = sb.tile([P, K], U8, align_bytes=64)
+        keys_plane = sb.tile([P, T], U8, align_bytes=64)
+        notes_plane = sb.tile([P, U], U8, align_bytes=64)
+        f1 = sb.tile([P, U], F32)
+        f2 = sb.tile([P, T], F32)
+        nc.vector.memset(wq_plane[:].bitcast(I32), 0)
+        nc.vector.memset(keys_plane[:].bitcast(I32), 0)
+        nc.vector.memset(notes_plane[:].bitcast(I32), 0)
+        nc.vector.memset(f1[:], 0.0)
+        nc.vector.memset(f2[:], 0.0)
+
+        states_raw = sb.tile([P, PACK, Q], F32)
+        wq_raw = sb.tile([P, K], U32)
+        keys_codes = sb.tile([P, T], U32, align_bytes=64)
+        notes_codes = sb.tile([P, 2 * U], U8, align_bytes=64)
+        lam_col = sb.tile([P, 1], F32)
+        lists = [sb.tile([P, SLOTS // 16], U16, name=f"list{n}") for n in range(5)]
+
+        load_scale_rows(nc.scalar, wq_plane, wq_scales)
+        nc.sync.dma_start(out=states_raw[:], in_=states.rearrange("(p j) q -> p j q", j=PACK))
+        nc.sync.dma_start(out=wq_raw[:].bitcast(I32), in_=wq_words[0].rearrange("p c r -> p (c r)").bitcast(I32))
+        nc.sync.dma_start(out=keys_codes[:].bitcast(I32), in_=keys_words[0].rearrange("p c r -> p (c r)").bitcast(I32))
+        load_scale_rows(nc.sync, keys_plane, keys_scales)
+        nc.sync.dma_start(lists[0][:], offs)
+        nc.sync.dma_start(lists[1][:], offs2)
+        nc.sync.dma_start(out=notes_codes[:].bitcast(I32), in_=notes_words[0].bitcast(I32))
+        load_scale_rows(nc.sync, notes_plane, notes_scales)
+        nc.sync.dma_start(lists[2][:], offs3)
+        nc.sync.dma_start(lists[3][:], offs4)
+        nc.sync.dma_start(out=lam_col[:], in_=lam)
+        nc.sync.dma_start(lists[4][:], offs5)
+
+        wq_plane_dealt = sb.tile([P, PACK, P], U8, align_bytes=64)
+        nc.vector.tensor_copy(
+            out=wq_plane_dealt[:].rearrange("p t m -> p m t"), in_=wq_plane[:].rearrange("p (m t) -> p m t", t=PACK)
+        )
+
+        states_bf = sb.tile([P, Q, PACK], BF16, align_bytes=64)
+        by_query = states_raw[:].rearrange("p j q -> p q j")
+        nc.vector.tensor_copy(out=states_bf[:, :STATES_ON_VECTOR, :], in_=by_query[:, :STATES_ON_VECTOR, :])
+        nc.scalar.activation(states_bf[:, STATES_ON_VECTOR:, :], by_query[:, STATES_ON_VECTOR:, :], COPY)
+        states_codes = sb.tile([P, Q], U32, align_bytes=64)
+        states_plane = sb.tile([P, Q], U8, align_bytes=64)
+        nc.vector.quantize_mx(
+            out=states_codes[:].bitcast(FP8X4), scales=states_plane[:], in_=states_bf[:].rearrange("p q j -> p (q j)")
+        )
+
+        wq_dealt = sb.tile([P, PACK, P], U32, align_bytes=64)
+        nc.scalar.copy(out=wq_dealt[:].rearrange("p t m -> p m t"), in_=wq_raw[:].rearrange("p (m t) -> p m t", t=PACK))
+
+        qv_ps = ps.tile([P, PACK, Q], F32)
+        for t in range(PACK):
+            nc.tensor.matmul_mx(
+                out=qv_ps[:, t, :],
+                lhsT=wq_dealt[:, t, :].bitcast(FP8X4),
+                lhsT_scale=wq_plane_dealt[:, t, :],
+                rhs=states_codes[:].bitcast(FP8X4),
+                rhs_scale=states_plane[:],
+                start=True,
+                stop=True,
+            )
+        qv_bf = sb.tile([P, Q, PACK], BF16, align_bytes=64)
+        nc.scalar.copy(out=qv_bf[:], in_=qv_ps[:].rearrange("p t q -> p q t"))
+        qv_codes = sb.tile([P, Q], U32, align_bytes=64)
+        qv_plane = sb.tile([P, Q], U8, align_bytes=64)
+        nc.vector.quantize_mx(out=qv_codes[:].bitcast(FP8X4), scales=qv_plane[:], in_=qv_bf[:].rearrange("p q t -> p (q t)"))
+
+        a = sb.tile([P, T], F32)
+        for c in range(T // A_COLS):
+            cols = slice(c * A_COLS, (c + 1) * A_COLS)
+            a_ps = ps.tile([P, A_COLS], F32, name=f"a_ps{c}")
+            nc.tensor.matmul_mx(
+                out=a_ps[:],
+                lhsT=qv_codes[:].bitcast(FP8X4),
+                lhsT_scale=qv_plane[:],
+                rhs=keys_codes[:, cols].bitcast(FP8X4),
+                rhs_scale=keys_plane[:, cols],
+                start=True,
+                stop=True,
+            )
+            if c % 2 == 0:
+                nc.scalar.copy(out=a[:, cols], in_=a_ps[:])
+            else:
+                nc.vector.tensor_copy(out=a[:, cols], in_=a_ps[:])
+
+        b_banks = []
+        for c in range(U // B_COLS):
+            b_ps = ps.tile([P, B_COLS], F32, name=f"b_ps{c}")
+            nc.tensor.matmul_mx(
+                out=b_ps[:],
+                lhsT=qv_codes[:].bitcast(FP8X4),
+                lhsT_scale=qv_plane[:],
+                rhs=notes_codes[:, 2 * c * B_COLS : 2 * (c + 1) * B_COLS].bitcast(FP4X4),
+                rhs_scale=notes_plane[:, c * B_COLS : (c + 1) * B_COLS],
+                start=True,
+                stop=True,
+            )
+            b_banks.append(b_ps)
+
+        def look_up(window, offsets, name):
+            first = sb.tile([P, HALF], F32, name=name + "_first")
+            second = sb.tile([P, HALF], F32, name=name + "_second")
+            nc.vector.tensor_copy(first[:], window[:].indirect(offsets[:, :HALF_COLS]))
+            nc.scalar.activation(second[:], window[:].indirect(offsets[:, HALF_COLS:]), COPY)
+            return first, second
+
+        def put(window, offsets, first, second):
+            nc.vector.tensor_copy(window[:].indirect(offsets[:, :HALF_COLS]), first[:])
+            nc.vector.tensor_copy(window[:].indirect(offsets[:, HALF_COLS:]), second[:])
+
+        put(f1, lists[1], *look_up(a, lists[0], "a_picked"))
+        cc = sb.tile([P, U], F32)
+        for c in range(U // B_COLS):
+            cols = slice(c * B_COLS, (c + 1) * B_COLS)
+            nc.vector.tensor_tensor(cc[:, cols], b_banks[c][:], f1[:, cols], ADD)
+
+        put(f2, lists[3], *look_up(cc, lists[2], "cc_picked"))
+        dd = sb.tile([P, T], F32)
+        nc.vector.scalar_tensor_tensor(dd[:], f2[:], lam_col[:], a[:], MULT, ADD)
+
+        first, second = look_up(dd, lists[4], "dd_picked")
+        nc.sync.dma_start(out=out[:, :HALF], in_=first[:])
+        nc.scalar.dma_start(out=out[:, HALF:], in_=second[:])

@@ -21,17 +21,19 @@ P = 128
 PACK = 4
 HALF = SLOTS // 2
 HALF_COLS = HALF // 16
-A_COLS = 256
+A_WIDTHS = (256, 256, 256, 128, 128)
+ADD_ON_VECTOR = 768
+WQ_ON_VECTOR = 64
 B_COLS = 512
 STATES_ON_VECTOR = 96
 
 
-def load_scale_rows(queue, plane, scales):
-    for quad in range(4):
-        queue.dma_start(
-            out=plane[32 * quad : 32 * quad + 4, :].bitcast(I32),
-            in_=scales[0, 4 * quad : 4 * quad + 4, :].bitcast(I32),
-        )
+def load_scale_rows(queue, plane, scales, quad, copies):
+    rows = scales[0, 4 * quad : 4 * quad + 4, :].bitcast(I32)
+    queue.dma_start(
+        out=plane[32 * quad : 32 * quad + 4 * copies, :].bitcast(I32),
+        in_=rows.unsqueeze(0).broadcast_to([copies, 4, plane.shape[1] // 4]),
+    )
 
 
 def tile_attend_thereandback_madetwo_kernel(
@@ -46,29 +48,27 @@ def tile_attend_thereandback_madetwo_kernel(
         keys_plane = sb.tile([P, T], U8, align_bytes=64)
         notes_plane = sb.tile([P, U], U8, align_bytes=64)
         f1 = sb.tile([P, U], F32)
-        f2 = sb.tile([P, T], F32)
-        nc.vector.memset(wq_plane[:].bitcast(I32), 0)
-        nc.vector.memset(keys_plane[:].bitcast(I32), 0)
-        nc.vector.memset(notes_plane[:].bitcast(I32), 0)
-        nc.vector.memset(f1[:], 0.0)
-        nc.vector.memset(f2[:], 0.0)
+        nc.vector.memset(f1[:].bitcast(I32), 0)
 
         states_raw = sb.tile([P, PACK, Q], F32)
-        wq_raw = sb.tile([P, K], U32)
+        wq_raw = sb.tile([P, K], U32, tag="wq_then_f2")
         keys_codes = sb.tile([P, T], U32, align_bytes=64)
         notes_codes = sb.tile([P, 2 * U], U8, align_bytes=64)
         lam_col = sb.tile([P, 1], F32)
         lists = [sb.tile([P, SLOTS // 16], U16, name=f"list{n}") for n in range(5)]
 
-        load_scale_rows(nc.scalar, wq_plane, wq_scales)
         nc.sync.dma_start(out=states_raw[:], in_=states.rearrange("(p j) q -> p j q", j=PACK))
+        for quad in range(4):
+            load_scale_rows(nc.scalar if quad < 2 else nc.sync, wq_plane, wq_scales, quad, 8)
         nc.sync.dma_start(out=wq_raw[:].bitcast(I32), in_=wq_words[0].rearrange("p c r -> p (c r)").bitcast(I32))
         nc.sync.dma_start(out=keys_codes[:].bitcast(I32), in_=keys_words[0].rearrange("p c r -> p (c r)").bitcast(I32))
-        load_scale_rows(nc.sync, keys_plane, keys_scales)
+        for quad in range(4):
+            load_scale_rows(nc.sync, keys_plane, keys_scales, quad, 8)
         nc.sync.dma_start(lists[0][:], offs)
         nc.sync.dma_start(lists[1][:], offs2)
         nc.sync.dma_start(out=notes_codes[:].bitcast(I32), in_=notes_words[0].bitcast(I32))
-        load_scale_rows(nc.sync, notes_plane, notes_scales)
+        for quad in range(4):
+            load_scale_rows(nc.sync, notes_plane, notes_scales, quad, 8)
         nc.sync.dma_start(lists[2][:], offs3)
         nc.sync.dma_start(lists[3][:], offs4)
         nc.sync.dma_start(out=lam_col[:], in_=lam)
@@ -90,7 +90,13 @@ def tile_attend_thereandback_madetwo_kernel(
         )
 
         wq_dealt = sb.tile([P, PACK, P], U32, align_bytes=64)
-        nc.scalar.copy(out=wq_dealt[:].rearrange("p t m -> p m t"), in_=wq_raw[:].rearrange("p (m t) -> p m t", t=PACK))
+        deal_to = wq_dealt[:].rearrange("p t m -> p m t")
+        deal_from = wq_raw[:].rearrange("p (m t) -> p m t", t=PACK)
+        nc.vector.tensor_copy(out=deal_to[:, :WQ_ON_VECTOR, :], in_=deal_from[:, :WQ_ON_VECTOR, :])
+        nc.scalar.copy(out=deal_to[:, WQ_ON_VECTOR:, :], in_=deal_from[:, WQ_ON_VECTOR:, :])
+
+        f2 = sb.tile([P, T], F32, tag="wq_then_f2")
+        nc.vector.memset(f2[:].bitcast(I32), 0)
 
         qv_ps = ps.tile([P, PACK, Q], F32)
         for t in range(PACK):
@@ -110,9 +116,11 @@ def tile_attend_thereandback_madetwo_kernel(
         nc.vector.quantize_mx(out=qv_codes[:].bitcast(FP8X4), scales=qv_plane[:], in_=qv_bf[:].rearrange("p q t -> p (q t)"))
 
         a = sb.tile([P, T], F32)
-        for c in range(T // A_COLS):
-            cols = slice(c * A_COLS, (c + 1) * A_COLS)
-            a_ps = ps.tile([P, A_COLS], F32, name=f"a_ps{c}")
+        a_banks = []
+        for c, width in enumerate(A_WIDTHS):
+            cols = slice(sum(A_WIDTHS[:c]), sum(A_WIDTHS[: c + 1]))
+            a_ps = ps.tile([P, width], F32, name=f"a_ps{c}")
+            a_banks.append((cols, a_ps))
             nc.tensor.matmul_mx(
                 out=a_ps[:],
                 lhsT=qv_codes[:].bitcast(FP8X4),
@@ -141,27 +149,34 @@ def tile_attend_thereandback_madetwo_kernel(
             )
             b_banks.append(b_ps)
 
-        def look_up(window, offsets, name):
-            first = sb.tile([P, HALF], F32, name=name + "_first")
-            second = sb.tile([P, HALF], F32, name=name + "_second")
-            nc.vector.tensor_copy(first[:], window[:].indirect(offsets[:, :HALF_COLS]))
-            nc.scalar.activation(second[:], window[:].indirect(offsets[:, HALF_COLS:]), COPY)
-            return first, second
+        b_tail = sb.tile([P, U - ADD_ON_VECTOR], F32)
+        nc.scalar.copy(out=b_tail[:], in_=b_banks[1][:, ADD_ON_VECTOR - B_COLS :])
+        lam_row = sb.tile([P, SLOTS], F32)
+        nc.scalar.copy(out=lam_row[:], in_=lam_col[:].to_broadcast([P, SLOTS]))
 
-        def put(window, offsets, first, second):
-            nc.vector.tensor_copy(window[:].indirect(offsets[:, :HALF_COLS]), first[:])
-            nc.vector.tensor_copy(window[:].indirect(offsets[:, HALF_COLS:]), second[:])
+        def look_up(picked, window, offsets):
+            nc.vector.tensor_copy(picked[:, :HALF], window[:].indirect(offsets[:, :HALF_COLS]))
+            nc.scalar.activation(picked[:, HALF:], window[:].indirect(offsets[:, HALF_COLS:]), COPY)
 
-        put(f1, lists[1], *look_up(a, lists[0], "a_picked"))
+        a_picked = sb.tile([P, SLOTS], F32)
+        look_up(a_picked, a, lists[0])
+        nc.vector.tensor_copy(f1[:].indirect(lists[1][:]), a_picked[:])
         cc = sb.tile([P, U], F32)
-        for c in range(U // B_COLS):
-            cols = slice(c * B_COLS, (c + 1) * B_COLS)
-            nc.vector.tensor_tensor(cc[:, cols], b_banks[c][:], f1[:, cols], ADD)
+        nc.vector.tensor_tensor(cc[:, :B_COLS], b_banks[0][:], f1[:, :B_COLS], ADD)
+        nc.vector.tensor_tensor(
+            cc[:, B_COLS:ADD_ON_VECTOR], b_banks[1][:, : ADD_ON_VECTOR - B_COLS], f1[:, B_COLS:ADD_ON_VECTOR], ADD
+        )
+        nc.gpsimd.tensor_tensor(cc[:, ADD_ON_VECTOR:], b_tail[:], f1[:, ADD_ON_VECTOR:], ADD)
 
-        put(f2, lists[3], *look_up(cc, lists[2], "cc_picked"))
+        cc_picked = sb.tile([P, SLOTS], F32)
+        look_up(cc_picked, cc, lists[2])
+        nc.vector.tensor_tensor(f2[:].indirect(lists[3][:]), cc_picked[:], lam_row[:], MULT)
         dd = sb.tile([P, T], F32)
-        nc.vector.scalar_tensor_tensor(dd[:], f2[:], lam_col[:], a[:], MULT, ADD)
+        for cols, a_ps in a_banks[:3]:
+            nc.vector.tensor_tensor(dd[:, cols], a_ps[:], f2[:, cols], ADD)
+        nc.gpsimd.tensor_tensor(dd[:, ADD_ON_VECTOR:], a[:, ADD_ON_VECTOR:], f2[:, ADD_ON_VECTOR:], ADD)
 
-        first, second = look_up(dd, lists[4], "dd_picked")
-        nc.sync.dma_start(out=out[:, :HALF], in_=first[:])
-        nc.scalar.dma_start(out=out[:, HALF:], in_=second[:])
+        dd_picked = sb.tile([P, SLOTS], F32)
+        look_up(dd_picked, dd, lists[4])
+        nc.sync.dma_start(out=out[:, :HALF], in_=dd_picked[:, :HALF])
+        nc.scalar.dma_start(out=out[:, HALF:], in_=dd_picked[:, HALF:])

@@ -22,10 +22,10 @@ PACK = 4
 HALF = SLOTS // 2
 HALF_COLS = HALF // 16
 A_WIDTHS = (256, 256, 256, 128, 128)
-ADD_ON_VECTOR = 768
+ADD_ON_VECTOR = 688
 WQ_ON_VECTOR = 64
 B_COLS = 512
-STATES_ON_VECTOR = 96
+STATES_ON_VECTOR = 80
 
 
 def load_scale_rows(queue, plane, scales, quad, copies):
@@ -48,12 +48,14 @@ def tile_attend_thereandback_madetwo_kernel(
         keys_plane = sb.tile([P, T], U8, align_bytes=64)
         notes_plane = sb.tile([P, U], U8, align_bytes=64)
         f1 = sb.tile([P, U], F32)
-        nc.vector.memset(f1[:].bitcast(I32), 0)
+        f2 = sb.tile([P, T], F32)
+        nc.vector.memset(f1[:], 0.0)
+        nc.vector.memset(f2[:], 0.0)
 
         states_raw = sb.tile([P, PACK, Q], F32)
-        wq_raw = sb.tile([P, K], U32, tag="wq_then_f2")
+        wq_raw = sb.tile([P, K], U32)
         keys_codes = sb.tile([P, T], U32, align_bytes=64)
-        notes_codes = sb.tile([P, 2 * U], U8, align_bytes=64)
+        notes_codes = sb.tile([P, 2 * U], U8, align_bytes=64, tag="notes_then_lam")
         lam_col = sb.tile([P, 1], F32)
         lists = [sb.tile([P, SLOTS // 16], U16, name=f"list{n}") for n in range(5)]
 
@@ -66,12 +68,12 @@ def tile_attend_thereandback_madetwo_kernel(
             load_scale_rows(nc.sync, keys_plane, keys_scales, quad, 8)
         nc.sync.dma_start(lists[0][:], offs)
         nc.sync.dma_start(lists[1][:], offs2)
+        nc.sync.dma_start(out=lam_col[:], in_=lam)
         nc.sync.dma_start(out=notes_codes[:].bitcast(I32), in_=notes_words[0].bitcast(I32))
         for quad in range(4):
             load_scale_rows(nc.sync, notes_plane, notes_scales, quad, 8)
         nc.sync.dma_start(lists[2][:], offs3)
         nc.sync.dma_start(lists[3][:], offs4)
-        nc.sync.dma_start(out=lam_col[:], in_=lam)
         nc.sync.dma_start(lists[4][:], offs5)
 
         wq_plane_dealt = sb.tile([P, PACK, P], U8, align_bytes=64)
@@ -95,22 +97,25 @@ def tile_attend_thereandback_madetwo_kernel(
         nc.vector.tensor_copy(out=deal_to[:, :WQ_ON_VECTOR, :], in_=deal_from[:, :WQ_ON_VECTOR, :])
         nc.scalar.copy(out=deal_to[:, WQ_ON_VECTOR:, :], in_=deal_from[:, WQ_ON_VECTOR:, :])
 
-        f2 = sb.tile([P, T], F32, tag="wq_then_f2")
-        nc.vector.memset(f2[:].bitcast(I32), 0)
-
-        qv_ps = ps.tile([P, PACK, Q], F32)
-        for t in range(PACK):
-            nc.tensor.matmul_mx(
-                out=qv_ps[:, t, :],
-                lhsT=wq_dealt[:, t, :].bitcast(FP8X4),
-                lhsT_scale=wq_plane_dealt[:, t, :],
-                rhs=states_codes[:].bitcast(FP8X4),
-                rhs_scale=states_plane[:],
-                start=True,
-                stop=True,
-            )
         qv_bf = sb.tile([P, Q, PACK], BF16, align_bytes=64)
-        nc.scalar.copy(out=qv_bf[:], in_=qv_ps[:].rearrange("p t q -> p q t"))
+        for pair in range(2):
+            qv_ps = ps.tile([P, 2, Q], F32, tag=f"qv_then_b{pair}")
+            for e in range(2):
+                t = 2 * pair + e
+                nc.tensor.matmul_mx(
+                    out=qv_ps[:, e, :],
+                    lhsT=wq_dealt[:, t, :].bitcast(FP8X4),
+                    lhsT_scale=wq_plane_dealt[:, t, :],
+                    rhs=states_codes[:].bitcast(FP8X4),
+                    rhs_scale=states_plane[:],
+                    start=True,
+                    stop=True,
+                )
+            places = qv_bf[:, :, 2 * pair : 2 * pair + 2]
+            if pair == 0:
+                nc.vector.tensor_copy(out=places, in_=qv_ps[:].rearrange("p e q -> p q e"))
+            else:
+                nc.scalar.copy(out=places, in_=qv_ps[:].rearrange("p e q -> p q e"))
         qv_codes = sb.tile([P, Q], U32, align_bytes=64)
         qv_plane = sb.tile([P, Q], U8, align_bytes=64)
         nc.vector.quantize_mx(out=qv_codes[:].bitcast(FP8X4), scales=qv_plane[:], in_=qv_bf[:].rearrange("p q t -> p (q t)"))
@@ -137,7 +142,7 @@ def tile_attend_thereandback_madetwo_kernel(
 
         b_banks = []
         for c in range(U // B_COLS):
-            b_ps = ps.tile([P, B_COLS], F32, name=f"b_ps{c}")
+            b_ps = ps.tile([P, B_COLS], F32, tag=f"qv_then_b{c}")
             nc.tensor.matmul_mx(
                 out=b_ps[:],
                 lhsT=qv_codes[:].bitcast(FP8X4),
@@ -149,17 +154,16 @@ def tile_attend_thereandback_madetwo_kernel(
             )
             b_banks.append(b_ps)
 
-        b_tail = sb.tile([P, U - ADD_ON_VECTOR], F32)
-        nc.scalar.copy(out=b_tail[:], in_=b_banks[1][:, ADD_ON_VECTOR - B_COLS :])
-        lam_row = sb.tile([P, SLOTS], F32)
-        nc.scalar.copy(out=lam_row[:], in_=lam_col[:].to_broadcast([P, SLOTS]))
-
         def look_up(picked, window, offsets):
             nc.vector.tensor_copy(picked[:, :HALF], window[:].indirect(offsets[:, :HALF_COLS]))
             nc.scalar.activation(picked[:, HALF:], window[:].indirect(offsets[:, HALF_COLS:]), COPY)
 
         a_picked = sb.tile([P, SLOTS], F32)
         look_up(a_picked, a, lists[0])
+        b_tail = sb.tile([P, U - ADD_ON_VECTOR], F32)
+        nc.scalar.copy(out=b_tail[:], in_=b_banks[1][:, ADD_ON_VECTOR - B_COLS :])
+        lam_row = sb.tile([P, SLOTS], F32, align_bytes=64, tag="notes_then_lam")
+        nc.scalar.copy(out=lam_row[:], in_=lam_col[:].to_broadcast([P, SLOTS]))
         nc.vector.tensor_copy(f1[:].indirect(lists[1][:]), a_picked[:])
         cc = sb.tile([P, U], F32)
         nc.vector.tensor_tensor(cc[:, :B_COLS], b_banks[0][:], f1[:, :B_COLS], ADD)
@@ -172,8 +176,10 @@ def tile_attend_thereandback_madetwo_kernel(
         look_up(cc_picked, cc, lists[2])
         nc.vector.tensor_tensor(f2[:].indirect(lists[3][:]), cc_picked[:], lam_row[:], MULT)
         dd = sb.tile([P, T], F32)
-        for cols, a_ps in a_banks[:3]:
-            nc.vector.tensor_tensor(dd[:, cols], a_ps[:], f2[:, cols], ADD)
+        for cols, a_ps in a_banks:
+            stop = min(cols.stop, ADD_ON_VECTOR)
+            if cols.start < stop:
+                nc.vector.tensor_tensor(dd[:, cols.start : stop], a_ps[:, : stop - cols.start], f2[:, cols.start : stop], ADD)
         nc.gpsimd.tensor_tensor(dd[:, ADD_ON_VECTOR:], a[:, ADD_ON_VECTOR:], f2[:, ADD_ON_VECTOR:], ADD)
 
         dd_picked = sb.tile([P, SLOTS], F32)

@@ -19,20 +19,24 @@ ADD = mybir.AluOpType.add
 
 P = 128
 PACK = 4
+QUADRANTS = 4
+QUADRANT = P // QUADRANTS
+SCALE_ROWS = 4
 HALF = SLOTS // 2
 HALF_COLS = HALF // 16
-A_WIDTHS = (256, 256, 256, 128, 128)
-ADD_ON_VECTOR = 688
-WQ_ON_VECTOR = 64
 B_COLS = 512
+
+A_WIDTHS = (256, 256, 256, 128, 128)
 STATES_ON_VECTOR = 80
+WQ_ON_VECTOR = 64
+ADD_ON_VECTOR = 672
 
 
-def load_scale_rows(queue, plane, scales, quad, copies):
-    rows = scales[0, 4 * quad : 4 * quad + 4, :].bitcast(I32)
+def load_scale_rows(queue, plane, scales, quad):
+    rows = scales[0, SCALE_ROWS * quad : SCALE_ROWS * (quad + 1), :].bitcast(I32)
     queue.dma_start(
-        out=plane[32 * quad : 32 * quad + 4 * copies, :].bitcast(I32),
-        in_=rows.unsqueeze(0).broadcast_to([copies, 4, plane.shape[1] // 4]),
+        out=plane[QUADRANT * quad : QUADRANT * (quad + 1), :].bitcast(I32),
+        in_=rows.unsqueeze(0).broadcast_to([QUADRANT // SCALE_ROWS, SCALE_ROWS, plane.shape[1] // 4]),
     )
 
 
@@ -47,6 +51,7 @@ def tile_attend_thereandback_madetwo_kernel(
         wq_plane = sb.tile([P, K], U8, align_bytes=64)
         keys_plane = sb.tile([P, T], U8, align_bytes=64)
         notes_plane = sb.tile([P, U], U8, align_bytes=64)
+
         f1 = sb.tile([P, U], F32)
         f2 = sb.tile([P, T], F32)
         nc.vector.memset(f1[:], 0.0)
@@ -60,26 +65,24 @@ def tile_attend_thereandback_madetwo_kernel(
         lists = [sb.tile([P, SLOTS // 16], U16, name=f"list{n}") for n in range(5)]
 
         nc.sync.dma_start(out=states_raw[:], in_=states.rearrange("(p j) q -> p j q", j=PACK))
-        for quad in range(4):
-            load_scale_rows(nc.scalar if quad < 2 else nc.sync, wq_plane, wq_scales, quad, 8)
+        for quad in range(QUADRANTS):
+            load_scale_rows(nc.scalar if quad < QUADRANTS // 2 else nc.sync, wq_plane, wq_scales, quad)
         nc.sync.dma_start(out=wq_raw[:].bitcast(I32), in_=wq_words[0].rearrange("p c r -> p (c r)").bitcast(I32))
         nc.sync.dma_start(out=keys_codes[:].bitcast(I32), in_=keys_words[0].rearrange("p c r -> p (c r)").bitcast(I32))
-        for quad in range(4):
-            load_scale_rows(nc.sync, keys_plane, keys_scales, quad, 8)
+        for quad in range(QUADRANTS):
+            load_scale_rows(nc.sync, keys_plane, keys_scales, quad)
         nc.sync.dma_start(lists[0][:], offs)
         nc.sync.dma_start(lists[1][:], offs2)
         nc.sync.dma_start(out=lam_col[:], in_=lam)
         nc.sync.dma_start(out=notes_codes[:].bitcast(I32), in_=notes_words[0].bitcast(I32))
-        for quad in range(4):
-            load_scale_rows(nc.sync, notes_plane, notes_scales, quad, 8)
+        for quad in range(QUADRANTS):
+            load_scale_rows(nc.sync, notes_plane, notes_scales, quad)
         nc.sync.dma_start(lists[2][:], offs3)
         nc.sync.dma_start(lists[3][:], offs4)
         nc.sync.dma_start(lists[4][:], offs5)
 
         wq_plane_dealt = sb.tile([P, PACK, P], U8, align_bytes=64)
-        nc.vector.tensor_copy(
-            out=wq_plane_dealt[:].rearrange("p t m -> p m t"), in_=wq_plane[:].rearrange("p (m t) -> p m t", t=PACK)
-        )
+        nc.vector.tensor_copy(out=wq_plane_dealt[:], in_=wq_plane[:].rearrange("p (m t) -> p t m", t=PACK))
 
         states_bf = sb.tile([P, Q, PACK], BF16, align_bytes=64)
         by_query = states_raw[:].rearrange("p j q -> p q j")
@@ -154,16 +157,18 @@ def tile_attend_thereandback_madetwo_kernel(
             )
             b_banks.append(b_ps)
 
-        def look_up(picked, window, offsets):
-            nc.vector.tensor_copy(picked[:, :HALF], window[:].indirect(offsets[:, :HALF_COLS]))
-            nc.scalar.activation(picked[:, HALF:], window[:].indirect(offsets[:, HALF_COLS:]), COPY)
+        def look_up(picked, table, offsets):
+            nc.vector.tensor_copy(picked[:, :HALF], table[:].indirect(offsets[:, :HALF_COLS]))
+            nc.scalar.activation(picked[:, HALF:], table[:].indirect(offsets[:, HALF_COLS:]), COPY)
 
         a_picked = sb.tile([P, SLOTS], F32)
         look_up(a_picked, a, lists[0])
+
         b_tail = sb.tile([P, U - ADD_ON_VECTOR], F32)
         nc.scalar.copy(out=b_tail[:], in_=b_banks[1][:, ADD_ON_VECTOR - B_COLS :])
         lam_row = sb.tile([P, SLOTS], F32, align_bytes=64, tag="notes_then_lam")
         nc.scalar.copy(out=lam_row[:], in_=lam_col[:].to_broadcast([P, SLOTS]))
+
         nc.vector.tensor_copy(f1[:].indirect(lists[1][:]), a_picked[:])
         cc = sb.tile([P, U], F32)
         nc.vector.tensor_tensor(cc[:, :B_COLS], b_banks[0][:], f1[:, :B_COLS], ADD)

from contextlib import ExitStack

import concourse.mybir as mybir

D, K, T, U, SLOTS, Q = 512, 512, 1024, 1024, 512, 128
FLOPS = 2 * Q * (D * K + K * T + K * U)

F32 = mybir.dt.float32
BF16 = mybir.dt.bfloat16
I32 = mybir.dt.int32
U32 = mybir.dt.uint32
U16 = mybir.dt.uint16
U8 = mybir.dt.uint8
FP8X4 = mybir.dt.float8_e4m3fn_x4
FP4X4 = mybir.dt.float4_e2m1fn_x4
COPY = mybir.ActivationFunctionType.Copy
MULT = mybir.AluOpType.mult
ADD = mybir.AluOpType.add

P = 128
PACK = 4
QUADRANTS = 4
QUADRANT = P // QUADRANTS
SCALE_ROWS = 4
HALF = SLOTS // 2
HALF_COLS = HALF // 16
B_COLS = 512

A_WIDTHS = (256, 256, 256, 128, 128)
STATES_ON_VECTOR = 80
WQ_ON_VECTOR = 64
ADD_ON_VECTOR = 672


def load_scale_rows(queue, plane, scales, quad):
    rows = scales[0, SCALE_ROWS * quad : SCALE_ROWS * (quad + 1), :].bitcast(I32)
    queue.dma_start(
        out=plane[QUADRANT * quad : QUADRANT * (quad + 1), :].bitcast(I32),
        in_=rows.unsqueeze(0).broadcast_to([QUADRANT // SCALE_ROWS, SCALE_ROWS, plane.shape[1] // 4]),
    )


def tile_attend_thereandback_madetwo_kernel(
    tc, states, wq_words, wq_scales, keys_words, keys_scales, notes_words, notes_scales, lam, offs, offs2, offs3, offs4, offs5, out
):
    nc = tc.nc
    with ExitStack() as ctx:
        sb = ctx.enter_context(tc.tile_pool(name="sb", bufs=1))
        ps = ctx.enter_context(tc.psum_pool(name="ps", bufs=1))

        wq_plane = sb.tile([P, K], U8, align_bytes=64)
        keys_plane = sb.tile([P, T], U8, align_bytes=64)
        notes_plane = sb.tile([P, U], U8, align_bytes=64)

        f1 = sb.tile([P, U], F32)
        f2 = sb.tile([P, T], F32)
        nc.vector.memset(f1[:], 0.0)
        nc.vector.memset(f2[:], 0.0)

        states_raw = sb.tile([P, PACK, Q], F32)
        wq_raw = sb.tile([P, K], U32)
        keys_codes = sb.tile([P, T], U32, align_bytes=64)
        notes_codes = sb.tile([P, 2 * U], U8, align_bytes=64, tag="notes_then_lam")
        lam_col = sb.tile([P, 1], F32)
        lists = [sb.tile([P, SLOTS // 16], U16, name=f"list{n}") for n in range(5)]

        nc.sync.dma_start(out=states_raw[:], in_=states.rearrange("(p j) q -> p j q", j=PACK))
        for quad in range(QUADRANTS):
            load_scale_rows(nc.scalar if quad < QUADRANTS // 2 else nc.sync, wq_plane, wq_scales, quad)
        nc.sync.dma_start(out=wq_raw[:].bitcast(I32), in_=wq_words[0].rearrange("p c r -> p (c r)").bitcast(I32))
        nc.sync.dma_start(out=keys_codes[:].bitcast(I32), in_=keys_words[0].rearrange("p c r -> p (c r)").bitcast(I32))
        for quad in range(QUADRANTS):
            load_scale_rows(nc.sync, keys_plane, keys_scales, quad)
        nc.sync.dma_start(lists[0][:], offs)
        nc.sync.dma_start(lists[1][:], offs2)
        nc.sync.dma_start(out=lam_col[:], in_=lam)
        nc.sync.dma_start(out=notes_codes[:].bitcast(I32), in_=notes_words[0].bitcast(I32))
        for quad in range(QUADRANTS):
            load_scale_rows(nc.sync, notes_plane, notes_scales, quad)
        nc.sync.dma_start(lists[2][:], offs3)
        nc.sync.dma_start(lists[3][:], offs4)
        nc.sync.dma_start(lists[4][:], offs5)

        wq_plane_dealt = sb.tile([P, PACK, P], U8, align_bytes=64)
        nc.vector.tensor_copy(out=wq_plane_dealt[:], in_=wq_plane[:].rearrange("p (m t) -> p t m", t=PACK))

        states_bf = sb.tile([P, Q, PACK], BF16, align_bytes=64)
        by_query = states_raw[:].rearrange("p j q -> p q j")
        nc.vector.tensor_copy(out=states_bf[:, :STATES_ON_VECTOR, :], in_=by_query[:, :STATES_ON_VECTOR, :])
        nc.scalar.activation(states_bf[:, STATES_ON_VECTOR:, :], by_query[:, STATES_ON_VECTOR:, :], COPY)
        states_codes = sb.tile([P, Q], U32, align_bytes=64)
        states_plane = sb.tile([P, Q], U8, align_bytes=64)
        nc.vector.quantize_mx(
            out=states_codes[:].bitcast(FP8X4), scales=states_plane[:], in_=states_bf[:].rearrange("p q j -> p (q j)")
        )

        wq_dealt = sb.tile([P, PACK, P], U32, align_bytes=64)
        deal_to = wq_dealt[:].rearrange("p t m -> p m t")
        deal_from = wq_raw[:].rearrange("p (m t) -> p m t", t=PACK)
        nc.vector.tensor_copy(out=deal_to[:, :WQ_ON_VECTOR, :], in_=deal_from[:, :WQ_ON_VECTOR, :])
        nc.scalar.copy(out=deal_to[:, WQ_ON_VECTOR:, :], in_=deal_from[:, WQ_ON_VECTOR:, :])

        qv_bf = sb.tile([P, Q, PACK], BF16, align_bytes=64)
        for pair in range(2):
            qv_ps = ps.tile([P, 2, Q], F32, tag=f"qv_then_b{pair}")
            for e in range(2):
                t = 2 * pair + e
                nc.tensor.matmul_mx(
                    out=qv_ps[:, e, :],
                    lhsT=wq_dealt[:, t, :].bitcast(FP8X4),
                    lhsT_scale=wq_plane_dealt[:, t, :],
                    rhs=states_codes[:].bitcast(FP8X4),
                    rhs_scale=states_plane[:],
                    start=True,
                    stop=True,
                )
            places = qv_bf[:, :, 2 * pair : 2 * pair + 2]
            if pair == 0:
                nc.vector.tensor_copy(out=places, in_=qv_ps[:].rearrange("p e q -> p q e"))
            else:
                nc.scalar.copy(out=places, in_=qv_ps[:].rearrange("p e q -> p q e"))
        qv_codes = sb.tile([P, Q], U32, align_bytes=64)
        qv_plane = sb.tile([P, Q], U8, align_bytes=64)
        nc.vector.quantize_mx(out=qv_codes[:].bitcast(FP8X4), scales=qv_plane[:], in_=qv_bf[:].rearrange("p q t -> p (q t)"))

        a = sb.tile([P, T], F32)
        a_banks = []
        for c, width in enumerate(A_WIDTHS):
            cols = slice(sum(A_WIDTHS[:c]), sum(A_WIDTHS[: c + 1]))
            a_ps = ps.tile([P, width], F32, name=f"a_ps{c}")
            a_banks.append((cols, a_ps))
            nc.tensor.matmul_mx(
                out=a_ps[:],
                lhsT=qv_codes[:].bitcast(FP8X4),
                lhsT_scale=qv_plane[:],
                rhs=keys_codes[:, cols].bitcast(FP8X4),
                rhs_scale=keys_plane[:, cols],
                start=True,
                stop=True,
            )
            if c % 2 == 0:
                nc.scalar.copy(out=a[:, cols], in_=a_ps[:])
            else:
                nc.vector.tensor_copy(out=a[:, cols], in_=a_ps[:])

        b_banks = []
        for c in range(U // B_COLS):
            b_ps = ps.tile([P, B_COLS], F32, tag=f"qv_then_b{c}")
            nc.tensor.matmul_mx(
                out=b_ps[:],
                lhsT=qv_codes[:].bitcast(FP8X4),
                lhsT_scale=qv_plane[:],
                rhs=notes_codes[:, 2 * c * B_COLS : 2 * (c + 1) * B_COLS].bitcast(FP4X4),
                rhs_scale=notes_plane[:, c * B_COLS : (c + 1) * B_COLS],
                start=True,
                stop=True,
            )
            b_banks.append(b_ps)

        def look_up(picked, table, offsets):
            nc.vector.tensor_copy(picked[:, :HALF], table[:].indirect(offsets[:, :HALF_COLS]))
            nc.scalar.activation(picked[:, HALF:], table[:].indirect(offsets[:, HALF_COLS:]), COPY)

        a_picked = sb.tile([P, SLOTS], F32)
        look_up(a_picked, a, lists[0])

        b_tail = sb.tile([P, U - ADD_ON_VECTOR], F32)
        nc.scalar.copy(out=b_tail[:], in_=b_banks[1][:, ADD_ON_VECTOR - B_COLS :])
        lam_row = sb.tile([P, SLOTS], F32, align_bytes=64, tag="notes_then_lam")
        nc.scalar.copy(out=lam_row[:], in_=lam_col[:].to_broadcast([P, SLOTS]))

        nc.vector.tensor_copy(f1[:].indirect(lists[1][:]), a_picked[:])
        cc = sb.tile([P, U], F32)
        nc.vector.tensor_tensor(cc[:, :B_COLS], b_banks[0][:], f1[:, :B_COLS], ADD)
        nc.vector.tensor_tensor(
            cc[:, B_COLS:ADD_ON_VECTOR], b_banks[1][:, : ADD_ON_VECTOR - B_COLS], f1[:, B_COLS:ADD_ON_VECTOR], ADD
        )
        nc.gpsimd.tensor_tensor(cc[:, ADD_ON_VECTOR:], b_tail[:], f1[:, ADD_ON_VECTOR:], ADD)

        cc_picked = sb.tile([P, SLOTS], F32)
        look_up(cc_picked, cc, lists[2])
        nc.vector.tensor_tensor(f2[:].indirect(lists[3][:]), cc_picked[:], lam_row[:], MULT)
        dd = sb.tile([P, T], F32)
        for cols, a_ps in a_banks:
            stop = min(cols.stop, ADD_ON_VECTOR)
            if cols.start < stop:
                nc.vector.tensor_tensor(dd[:, cols.start : stop], a_ps[:, : stop - cols.start], f2[:, cols.start : stop], ADD)
        nc.gpsimd.tensor_tensor(dd[:, ADD_ON_VECTOR:], a[:, ADD_ON_VECTOR:], f2[:, ADD_ON_VECTOR:], ADD)

        dd_picked = sb.tile([P, SLOTS], F32)
        look_up(dd_picked, dd, lists[4])
        nc.sync.dma_start(out=out[:, :HALF], in_=dd_picked[:, :HALF])
        nc.scalar.dma_start(out=out[:, HALF:], in_=dd_picked[:, HALF:])
